import numpy as np
import ml_dtypes

BF16 = ml_dtypes.bfloat16


def bf(x):
    return np.asarray(x, np.float32).astype(BF16)


def f32(x):
    return np.asarray(x, np.float32)


def f64(x):
    return np.asarray(x).astype(np.float64)


def striped(idx):
    return np.tile(idx.reshape(-1, 16).T, (8, 1))


S, K, M, N, E, Q, O = 512, 128, 256, 384, 4, 96, 256


def gelu_tanh(v):
    return 0.5 * v * (1.0 + np.tanh(np.sqrt(2.0 / np.pi) * (v + 0.044715 * v**3)))


def setup_inputs():
    return {"base": bf(np.random.standard_normal((M, S))), "x": bf(np.random.standard_normal((K, N))), "w": bf(1.2 * np.random.standard_normal((E, K, M)) / np.sqrt(K)), "w2": bf(np.random.standard_normal((M, O)) / np.sqrt(2 * M)), "b": f32(0.5 * np.random.standard_normal((O, 1))), "offs": striped(np.random.permutation(S)[:N])}


def reference(base, x, w, w2, b, offs):
    idx = offs[:16].T.reshape(-1)
    z = f64(base).copy()
    for e in range(E):
        z[:, idx[e * Q : (e + 1) * Q]] += f64(w)[e].T @ f64(x)[:, e * Q : (e + 1) * Q]
    y = f64(w2).T @ z
    return gelu_tanh(y + f64(b))

@@ -1,0 +1,67 @@
+import concourse.mybir as mybir
+from concourse.masks import make_identity
+
+BF16, F32, U16 = mybir.dt.bfloat16, mybir.dt.float32, mybir.dt.uint16
+GELU = mybir.ActivationFunctionType.Gelu_apprx_tanh
+
+P = 128
+S, K, M, N, E, O = 512, 128, 256, 384, 4, 256
+Q = N // E
+M_BLOCKS, O_BLOCKS = M // P, O // P
+FLOPS = 2 * K * M * N + 2 * M * O * S
+
+
+def tile_rows_thenproj_gelu_kernel(tc, base, x, w, w2, b, offs, out):
+    nc = tc.nc
+    with (
+        tc.tile_pool(name="held", bufs=1) as held,
+        tc.psum_pool(name="psum", bufs=1) as psum,
+    ):
+        base_sb = held.tile([P, M_BLOCKS, S], BF16)
+        nc.sync.dma_start(base_sb[:], base.rearrange("(a p) s -> p a s", p=P))
+        offsets = held.tile([P, N // 16], U16)
+        nc.sync.dma_start(offsets[:], offs)
+        x_sb = held.tile([K, N], BF16)
+        nc.sync.dma_start(x_sb[:], x)
+        w_sb = held.tile([K, E, M], BF16)
+        nc.scalar.dma_start(w_sb[:], w.rearrange("e k m -> k e m"))
+        w2_sb = held.tile([P, M_BLOCKS, O], BF16)
+        nc.scalar.dma_start(w2_sb[:], w2.rearrange("(a p) o -> p a o", p=P))
+        b_sb = held.tile([P, O_BLOCKS], F32)
+        nc.scalar.dma_start(b_sb[:], b.rearrange("(a p) o -> p (a o)", p=P))
+
+        ident = held.tile([P, P], BF16)
+        make_identity(nc, ident[:])
+
+        windows = [psum.tile([P, S], F32, name=f"window{a}") for a in range(M_BLOCKS)]
+        for a in range(M_BLOCKS):
+            nc.tensor.matmul(windows[a][:], ident[:], base_sb[:, a, :], start=True, stop=False)
+
+        for a in range(M_BLOCKS):
+            for e in range(E):
+                nc.tensor.matmul(
+                    windows[a][:].indirect(offsets[:, e * Q // 16 : (e + 1) * Q // 16]),
+                    w_sb[:, e, a * P : (a + 1) * P],
+                    x_sb[:, e * Q : (e + 1) * Q],
+                    start=False,
+                    stop=e == E - 1,
+                )
+
+        z_sb = [held.tile([P, S], BF16, name=f"z{a}") for a in range(M_BLOCKS)]
+        nc.vector.tensor_copy(z_sb[0][:], windows[0][:])
+        nc.scalar.copy(z_sb[1][:], windows[1][:])
+
+        y = [psum.tile([P, S], F32, name=f"y{o}") for o in range(O_BLOCKS)]
+        for a in range(M_BLOCKS):
+            for o in range(O_BLOCKS):
+                nc.tensor.matmul(
+                    y[o][:],
+                    w2_sb[:, a, o * P : (o + 1) * P],
+                    z_sb[a][:],
+                    start=a == 0,
+                    stop=a == M_BLOCKS - 1,
+                )
+        for o in range(O_BLOCKS):
+            out_sb = held.tile([P, S], F32, name=f"out{o}")
+            nc.scalar.activation(out_sb[:], y[o][:], GELU, bias=b_sb[:, o : o + 1])
+            nc.sync.dma_start(out[o * P : (o + 1) * P, :], out_sb[:])

@@ -8,6 +8,8 @@ P = 128
 S, K, M, N, E, O = 512, 128, 256, 384, 4, 256
 Q = N // E
 M_BLOCKS, O_BLOCKS = M // P, O // P
+HALVES, HALF = 2, S // 2
+WARM_UPS = 12
 FLOPS = 2 * K * M * N + 2 * M * O * S
 
 
@@ -30,6 +32,14 @@ def tile_rows_thenproj_gelu_kernel(tc, base, x, w, w2, b, offs, out):
         b_sb = held.tile([P, O_BLOCKS], F32)
         nc.scalar.dma_start(b_sb[:], b.rearrange("(a p) o -> p (a o)", p=P))
 
+        zeros = held.tile([P, P], BF16)
+        nc.vector.memset(zeros[:], 0.0)
+        spare = psum.tile([P, P], F32)
+        for step in range(WARM_UPS):
+            nc.tensor.matmul(spare[:], zeros[:], zeros[:], start=True, stop=True)
+        warm_gelu = held.tile([P, 1], F32)
+        nc.scalar.activation(warm_gelu[:], zeros[:, :1], GELU)
+
         ident = held.tile([P, P], BF16)
         make_identity(nc, ident[:])
 
@@ -47,21 +57,27 @@ def tile_rows_thenproj_gelu_kernel(tc, base, x, w, w2, b, offs, out):
                     stop=e == E - 1,
                 )
 
-        z_sb = [held.tile([P, S], BF16, name=f"z{a}") for a in range(M_BLOCKS)]
-        nc.vector.tensor_copy(z_sb[0][:], windows[0][:])
-        nc.scalar.copy(z_sb[1][:], windows[1][:])
-
-        y = [psum.tile([P, S], F32, name=f"y{o}") for o in range(O_BLOCKS)]
+        z_sb = [
+            [held.tile([P, HALF], BF16, name=f"z{a}_{h}") for h in range(HALVES)] for a in range(M_BLOCKS)
+        ]
         for a in range(M_BLOCKS):
+            for h in range(HALVES):
+                nc.vector.tensor_copy(z_sb[a][h][:], windows[a][:, h * HALF : (h + 1) * HALF])
+
+        y = [[psum.tile([P, HALF], F32, name=f"y{o}_{h}") for h in range(HALVES)] for o in range(O_BLOCKS)]
+        for a in range(M_BLOCKS):
+            for h in range(HALVES):
+                for o in range(O_BLOCKS):
+                    nc.tensor.matmul(
+                        y[o][h][:],
+                        w2_sb[:, a, o * P : (o + 1) * P],
+                        z_sb[a][h][:],
+                        start=a == 0,
+                        stop=a == M_BLOCKS - 1,
+                    )
+
+        for h in range(HALVES):
             for o in range(O_BLOCKS):
-                nc.tensor.matmul(
-                    y[o][:],
-                    w2_sb[:, a, o * P : (o + 1) * P],
-                    z_sb[a][:],
-                    start=a == 0,
-                    stop=a == M_BLOCKS - 1,
-                )
-        for o in range(O_BLOCKS):
-            out_sb = held.tile([P, S], F32, name=f"out{o}")
-            nc.scalar.activation(out_sb[:], y[o][:], GELU, bias=b_sb[:, o : o + 1])
-            nc.sync.dma_start(out[o * P : (o + 1) * P, :], out_sb[:])
+                out_sb = held.tile([P, HALF], F32, name=f"out{o}_{h}")
+                nc.scalar.activation(out_sb[:], y[o][h][:], GELU, bias=b_sb[:, o : o + 1])
+                nc.sync.dma_start(out[o * P : (o + 1) * P, h * HALF : (h + 1) * HALF], out_sb[:])

@@ -21,16 +21,16 @@ def tile_rows_thenproj_gelu_kernel(tc, base, x, w, w2, b, offs, out):
     ):
         base_sb = held.tile([P, M_BLOCKS, S], BF16)
         nc.sync.dma_start(base_sb[:], base.rearrange("(a p) s -> p a s", p=P))
-        offsets = held.tile([P, N // 16], U16)
-        nc.sync.dma_start(offsets[:], offs)
         x_sb = held.tile([K, N], BF16)
         nc.sync.dma_start(x_sb[:], x)
+        offsets = held.tile([P, N // 16], U16)
+        nc.sync.dma_start(offsets[:], offs)
         w_sb = held.tile([K, E, M], BF16)
-        nc.scalar.dma_start(w_sb[:], w.rearrange("e k m -> k e m"))
+        nc.sync.dma_start(w_sb[:], w.rearrange("e k m -> k e m"))
         w2_sb = held.tile([P, M_BLOCKS, O], BF16)
-        nc.scalar.dma_start(w2_sb[:], w2.rearrange("(a p) o -> p a o", p=P))
+        nc.sync.dma_start(w2_sb[:], w2.rearrange("(a p) o -> p a o", p=P))
         b_sb = held.tile([P, O_BLOCKS], F32)
-        nc.scalar.dma_start(b_sb[:], b.rearrange("(a p) o -> p (a o)", p=P))
+        nc.sync.dma_start(b_sb[:], b.rearrange("(a p) o -> p (a o)", p=P))
 
         zeros = held.tile([P, P], BF16)
         nc.vector.memset(zeros[:], 0.0)

@@ -20,7 +20,7 @@ def tile_rows_thenproj_gelu_kernel(tc, base, x, w, w2, b, offs, out):
         tc.psum_pool(name="psum", bufs=1) as psum,
     ):
         base_sb = held.tile([P, M_BLOCKS, S], BF16)
-        nc.sync.dma_start(base_sb[:], base.rearrange("(a p) s -> p a s", p=P))
+        nc.sync.dma_start(base_sb[:], base.rearrange("(p a) s -> p a s", p=P))
         x_sb = held.tile([K, N], BF16)
         nc.sync.dma_start(x_sb[:], x)
         offsets = held.tile([P, N // 16], U16)
@@ -28,9 +28,9 @@ def tile_rows_thenproj_gelu_kernel(tc, base, x, w, w2, b, offs, out):
         w_sb = held.tile([K, E, M], BF16)
         nc.sync.dma_start(w_sb[:], w.rearrange("e k m -> k e m"))
         w2_sb = held.tile([P, M_BLOCKS, O], BF16)
-        nc.sync.dma_start(w2_sb[:], w2.rearrange("(a p) o -> p a o", p=P))
+        nc.sync.dma_start(w2_sb[:], w2.rearrange("(p a) o -> p a o", p=P))
         b_sb = held.tile([P, O_BLOCKS], F32)
-        nc.sync.dma_start(b_sb[:], b.rearrange("(a p) o -> p (a o)", p=P))
+        nc.sync.dma_start(b_sb[:], b.rearrange("(p a) o -> p (a o)", p=P))
 
         zeros = held.tile([P, P], BF16)
         nc.vector.memset(zeros[:], 0.0)
@@ -51,7 +51,7 @@ def tile_rows_thenproj_gelu_kernel(tc, base, x, w, w2, b, offs, out):
             for e in range(E):
                 nc.tensor.matmul(
                     windows[a][:].indirect(offsets[:, e * Q // 16 : (e + 1) * Q // 16]),
-                    w_sb[:, e, a * P : (a + 1) * P],
+                    w_sb[:, e, a::M_BLOCKS],
                     x_sb[:, e * Q : (e + 1) * Q],
                     start=False,
                     stop=e == E - 1,
@@ -70,14 +70,15 @@ def tile_rows_thenproj_gelu_kernel(tc, base, x, w, w2, b, offs, out):
                 for o in range(O_BLOCKS):
                     nc.tensor.matmul(
                         y[o][h][:],
-                        w2_sb[:, a, o * P : (o + 1) * P],
+                        w2_sb[:, a, o::O_BLOCKS],
                         z_sb[a][h][:],
                         start=a == 0,
                         stop=a == M_BLOCKS - 1,
                     )
 
+        out_blocks = out.rearrange("(p a) s -> p a s", p=P)
         for h in range(HALVES):
             for o in range(O_BLOCKS):
                 out_sb = held.tile([P, HALF], F32, name=f"out{o}_{h}")
                 nc.scalar.activation(out_sb[:], y[o][h][:], GELU, bias=b_sb[:, o : o + 1])
-                nc.sync.dma_start(out[o * P : (o + 1) * P, h * HALF : (h + 1) * HALF], out_sb[:])
+                nc.sync.dma_start(out_blocks[:, o, h * HALF : (h + 1) * HALF], out_sb[:])

@@ -9,7 +9,7 @@ S, K, M, N, E, O = 512, 128, 256, 384, 4, 256
 Q = N // E
 M_BLOCKS, O_BLOCKS = M // P, O // P
 HALVES, HALF = 2, S // 2
-WARM_UPS = 12
+WARM_UPS = 18
 FLOPS = 2 * K * M * N + 2 * M * O * S
 
 

import concourse.mybir as mybir
from concourse.masks import make_identity

BF16, F32, U16 = mybir.dt.bfloat16, mybir.dt.float32, mybir.dt.uint16
GELU = mybir.ActivationFunctionType.Gelu_apprx_tanh

P = 128
S, K, M, N, E, O = 512, 128, 256, 384, 4, 256
Q = N // E
M_BLOCKS, O_BLOCKS = M // P, O // P
HALVES, HALF = 2, S // 2
WARM_UPS = 18
FLOPS = 2 * K * M * N + 2 * M * O * S


def tile_rows_thenproj_gelu_kernel(tc, base, x, w, w2, b, offs, out):
    nc = tc.nc
    with (
        tc.tile_pool(name="held", bufs=1) as held,
        tc.psum_pool(name="psum", bufs=1) as psum,
    ):
        base_sb = held.tile([P, M_BLOCKS, S], BF16)
        nc.sync.dma_start(base_sb[:], base.rearrange("(p a) s -> p a s", p=P))
        x_sb = held.tile([K, N], BF16)
        nc.sync.dma_start(x_sb[:], x)
        offsets = held.tile([P, N // 16], U16)
        nc.sync.dma_start(offsets[:], offs)
        w_sb = held.tile([K, E, M], BF16)
        nc.sync.dma_start(w_sb[:], w.rearrange("e k m -> k e m"))
        w2_sb = held.tile([P, M_BLOCKS, O], BF16)
        nc.sync.dma_start(w2_sb[:], w2.rearrange("(p a) o -> p a o", p=P))
        b_sb = held.tile([P, O_BLOCKS], F32)
        nc.sync.dma_start(b_sb[:], b.rearrange("(p a) o -> p (a o)", p=P))

        zeros = held.tile([P, P], BF16)
        nc.vector.memset(zeros[:], 0.0)
        spare = psum.tile([P, P], F32)
        for step in range(WARM_UPS):
            nc.tensor.matmul(spare[:], zeros[:], zeros[:], start=True, stop=True)
        warm_gelu = held.tile([P, 1], F32)
        nc.scalar.activation(warm_gelu[:], zeros[:, :1], GELU)

        ident = held.tile([P, P], BF16)
        make_identity(nc, ident[:])

        windows = [psum.tile([P, S], F32, name=f"window{a}") for a in range(M_BLOCKS)]
        for a in range(M_BLOCKS):
            nc.tensor.matmul(windows[a][:], ident[:], base_sb[:, a, :], start=True, stop=False)

        for a in range(M_BLOCKS):
            for e in range(E):
                nc.tensor.matmul(
                    windows[a][:].indirect(offsets[:, e * Q // 16 : (e + 1) * Q // 16]),
                    w_sb[:, e, a::M_BLOCKS],
                    x_sb[:, e * Q : (e + 1) * Q],
                    start=False,
                    stop=e == E - 1,
                )

        z_sb = [
            [held.tile([P, HALF], BF16, name=f"z{a}_{h}") for h in range(HALVES)] for a in range(M_BLOCKS)
        ]
        for a in range(M_BLOCKS):
            for h in range(HALVES):
                nc.vector.tensor_copy(z_sb[a][h][:], windows[a][:, h * HALF : (h + 1) * HALF])

        y = [[psum.tile([P, HALF], F32, name=f"y{o}_{h}") for h in range(HALVES)] for o in range(O_BLOCKS)]
        for a in range(M_BLOCKS):
            for h in range(HALVES):
                for o in range(O_BLOCKS):
                    nc.tensor.matmul(
                        y[o][h][:],
                        w2_sb[:, a, o::O_BLOCKS],
                        z_sb[a][h][:],
                        start=a == 0,
                        stop=a == M_BLOCKS - 1,
                    )

        out_blocks = out.rearrange("(p a) s -> p a s", p=P)
        for h in range(HALVES):
            for o in range(O_BLOCKS):
                out_sb = held.tile([P, HALF], F32, name=f"out{o}_{h}")
                nc.scalar.activation(out_sb[:], y[o][h][:], GELU, bias=b_sb[:, o : o + 1])
                nc.sync.dma_start(out_blocks[:, o, h * HALF : (h + 1) * HALF], out_sb[:])
